import numpy as np
import ml_dtypes


def mxq(x, axis, fmt="e4m3"):
    dtype, down = {"e4m3": (ml_dtypes.float8_e4m3fn, 7), "e5m2": (ml_dtypes.float8_e5m2, 14)}[fmt]
    v = np.moveaxis(np.asarray(x, np.float32).astype(ml_dtypes.bfloat16).astype(np.float64), axis, -1)
    blocks = v.reshape(v.shape[:-1] + (-1, 32))
    amax = np.abs(blocks).max(-1, keepdims=True)
    byte = np.maximum(np.where(amax > 0, np.frexp(amax)[1] - 1 + 127, 0) - down, 1)
    scale = np.exp2(byte - 127.0)
    codes = (blocks / scale).astype(np.float32).astype(dtype).astype(np.float64)
    return np.moveaxis((codes * scale).reshape(v.shape), -1, axis)


WIDE = False


def mx_kscale(k):
    if not WIDE:
        return np.ones(k)
    levels = np.array([10, -10, 5, -5, 0])
    if k % 512:
        return np.exp2(np.random.permutation(np.resize(levels, k // 32))).repeat(32)
    a = np.empty((k // 512, 16))
    for p in range(k // 512):
        a[p, :8] = np.random.permutation(np.resize(levels, 8))
        for g in range(8):
            far = levels[np.abs(levels - a[p, g]) >= 10]
            a[p, g + 8] = far[np.random.randint(len(far))]
    return np.exp2(a.ravel()).repeat(32)


def f64(x):
    return np.asarray(x).astype(np.float64)


def striped(idx):
    return np.tile(idx.reshape(-1, 16).T, (8, 1)).astype(np.uint16)


def unstriped(offs):
    return offs[:16].T.reshape(-1).astype(np.int64)


def pack_weight(w):
    k, n = w.shape
    w = f64(np.asarray(w, np.float32).astype(ml_dtypes.bfloat16)).reshape(k // 32, 32, n)
    amax = np.abs(w).max(1)
    byte = np.clip(np.where(amax > 0, np.frexp(amax)[1] - 1 + 127 - 7, 1), 1, 254)
    scaled = (w * np.exp2(127.0 - byte)[:, None, :]).reshape(k, n).astype(np.float32)
    words = np.ascontiguousarray(scaled.reshape(k // 512, 128, 4, n).transpose(0, 1, 3, 2)).astype(ml_dtypes.float8_e4m3fn).view(np.uint8)
    return words, np.ascontiguousarray(byte.astype(np.uint8).reshape(k // 512, 16, n))


def unpack_weight(words, scales):
    g, p, n, _ = words.shape
    vals = np.ascontiguousarray(words).view(ml_dtypes.float8_e4m3fn).astype(np.float64) * np.repeat(np.exp2(scales.astype(np.float64) - 127.0), 8, axis=1)[..., None]
    return vals.transpose(0, 1, 3, 2).reshape(g * 512, n)


K, T, S, V, H, N = 1024, 2048, 768, 256, 512, 256


def setup_inputs():
    n = np.random.standard_normal
    s = mx_kscale(K)[:, None]
    u = mx_kscale(H)
    packed_xT = pack_weight(n((K, T)) * s)
    packed_w2 = pack_weight(n((H, N)) / np.sqrt(2 * H) / u[:, None])
    packed_w3 = pack_weight(n((H, N)) / np.sqrt(2 * H) / u[:, None])
    return {
        "x_words": packed_xT[0],
        "x_scales": packed_xT[1],
        "w1": (n((K, H)) / np.sqrt(K) / s * u).astype(np.float32),
        "w2_words": packed_w2[0],
        "w2_scales": packed_w2[1],
        "w3_words": packed_w3[0],
        "w3_scales": packed_w3[1],
        "offs": striped(np.random.permutation(T)[:S]),
    }


def reference(x_words, x_scales, w1, w2_words, w2_scales, w3_words, w3_scales, offs):
    xq = unpack_weight(x_words, x_scales)[:, unstriped(offs)]
    h = mxq(f64(w1), 0, "e4m3").T @ xq
    mean = (h[:, :V] + h[:, V:2 * V] + h[:, 2 * V:3 * V]) / 3
    dev = np.sqrt(((h[:, :V] - mean) ** 2 + (h[:, V:2 * V] - mean) ** 2 + (h[:, 2 * V:3 * V] - mean) ** 2) / 3)
    return unpack_weight(w2_words, w2_scales).T @ mxq(mean, 0, "e4m3") + unpack_weight(w3_words, w3_scales).T @ mxq(dev, 0, "e4m3")

@@ -1,0 +1,230 @@
+import math
+from contextlib import ExitStack
+
+import concourse.mybir as mybir
+
+K, T, S, V, H, N = 1024, 2048, 768, 256, 512, 256
+FLOPS = 2 * K * H * S + 2 * 2 * H * N * V
+
+F32 = mybir.dt.float32
+BF16 = mybir.dt.bfloat16
+I32 = mybir.dt.int32
+U32 = mybir.dt.uint32
+U16 = mybir.dt.uint16
+U8 = mybir.dt.uint8
+FP8X4 = mybir.dt.float8_e4m3fn_x4
+ACT = mybir.ActivationFunctionType
+ALU = mybir.AluOpType
+
+P = 128
+PACK = 4
+PASSES = K // (P * PACK)
+PIECES = S // V
+HALVES = V // P
+BANK = 512
+
+
+def tile_picked_statpool_none_p_kernel(
+    tc, x_words, x_scales, w1, w2_words, w2_scales, w3_words, w3_scales, offs, out
+):
+    nc = tc.nc
+    with ExitStack() as ctx:
+        keep = ctx.enter_context(tc.tile_pool(name="keep", bufs=1))
+        shared = ctx.enter_context(tc.tile_pool(name="shared", bufs=1))
+        psum = ctx.enter_context(tc.psum_pool(name="psum", bufs=1))
+
+        def placed(shape, dtype, name, offset):
+            return shared.tile(shape, dtype, name=name, align_bytes=64, offset=offset)
+
+        def ring_bank(name):
+            return psum.tile([P, BANK], F32, name=name, tag="ring", bufs=6)
+
+        offsets = keep.tile([P, S // 16], U16, name="offsets")
+        nc.sync.dma_start(offsets[:], offs)
+
+        x_tiles = [keep.tile([P, T], I32, name="x_tile0", align_bytes=64), placed([P, T], I32, "x_tile1", 2048)]
+        nc.sync.dma_start(x_tiles[0][:], x_words[0].rearrange("p n t -> p (n t)").bitcast(I32))
+
+        x_planes = keep.tile([P, T], U8, name="x_planes", tag="planes", align_bytes=64)
+        nc.gpsimd.memset(x_planes[:].bitcast(I32), 0)
+        for q in range(4):
+            nc.sync.dma_start(
+                x_planes[32 * q : 32 * q + 4 * PASSES, :].bitcast(I32),
+                x_scales[:, 4 * q : 4 * q + 4, :].bitcast(I32),
+            )
+
+        zeros = placed([P, P], F32, "zeros", 2048 + 4 * T - 256)
+        identity = keep.tile([P, P], F32, name="identity")
+        nc.gpsimd.memset(zeros[:], 0.0)
+        nc.gpsimd.affine_select(
+            out=identity[:], in_=zeros[:], compare_op=ALU.not_equal, fill=1.0, base=0, pattern=[[-1, P]], channel_multiplier=1
+        )
+        warm = keep.tile([P, 1], F32, name="warm")
+        nc.scalar.activation(warm[:], identity[:, 0:1], ACT.Sqrt)
+
+        nc.sync.dma_start(x_tiles[1][:], x_words[1].rearrange("p n t -> p (n t)").bitcast(I32))
+        raw_all = placed([P, PASSES * PACK * H], F32, "raw_all", 2048 + 4 * T)
+        chunks = ((0, 128), (128, 128), (256, 256))
+        raws = {}
+        for c, (start, width) in enumerate(chunks):
+            for z in range(PASSES):
+                at = PACK * (PASSES * start + z * width)
+                raws[(c, z)] = raw_all[:, at : at + PACK * width].rearrange("p (j n) -> p j n", j=PACK)
+                rows = w1[z * P * PACK : (z + 1) * P * PACK, start : start + width]
+                nc.sync.dma_start(raws[(c, z)], rows.rearrange("(p j) n -> p j n", j=PACK))
+
+        picked_planes = keep.tile([P, S], U8, name="picked_planes", align_bytes=64)
+        picked = [
+            keep.tile([P, S], U32, name="picked0", align_bytes=64),
+            keep.tile([P, S], U32, name="picked1", tag="planes", align_bytes=64),
+        ]
+        nc.vector.tensor_copy(picked[0][:], x_tiles[0][:].bitcast(U32).indirect(offsets[:]))
+        nc.vector.tensor_copy(picked_planes[:], x_planes[:].indirect(offsets[:]))
+        nc.vector.tensor_copy(picked[1][:], x_tiles[1][:].bitcast(U32).indirect(offsets[:]))
+
+        last_words = []
+        for g, words in enumerate((w2_words, w3_words)):
+            tile = placed([P, N], I32, "last_words%d" % g, 7168 + 1024 * g)
+            nc.sync.dma_start(tile[:], words[0].rearrange("p n t -> p (n t)").bitcast(I32))
+            last_words.append(tile)
+        last_planes = placed([P, N], U8, "last_planes", 9216)
+        nc.gpsimd.memset(last_planes[:].bitcast(I32), 0)
+        for g, scales in enumerate((w2_scales, w3_scales)):
+            for q in range(4):
+                nc.sync.dma_start(
+                    last_planes[32 * q + 4 * g : 32 * q + 4 * g + 4, :].bitcast(I32),
+                    scales[0, 4 * q : 4 * q + 4, :].bitcast(I32),
+                )
+
+        def interleave(copy, grouped, raw):
+            copy(grouped.rearrange("p (b i) j -> p b j i", i=4), raw.rearrange("p j (b i) -> p b j i", i=4))
+
+        def quantize(codes, planes, values):
+            nc.vector.quantize_mx(out=codes.bitcast(FP8X4), scales=planes, in_=values.rearrange("p n j -> p (n j)"))
+
+        mean_rows = keep.tile([P, HALVES, H], BF16, name="mean_rows", align_bytes=64)
+        squares = [keep.tile([P, HALVES, PACK, P], F32, name="squares%d" % i) for i in range(2)]
+
+        def pool_stats(name, codes, planes, start, width, halves):
+            count = len(halves)
+            h = []
+            for d in range(PIECES):
+                view = ring_bank("h%s_%d" % (name, d))[:, : count * width].rearrange("p (a n) -> p a n", a=count)
+                for i, a in enumerate(halves):
+                    cols = slice(d * V + a * P, d * V + (a + 1) * P)
+                    for z in range(PASSES):
+                        nc.tensor.matmul_mx(
+                            out=view[:, i, :],
+                            lhsT=picked[z][:, cols].bitcast(FP8X4),
+                            lhsT_scale=picked_planes[4 * z : P, cols],
+                            rhs=codes[z].bitcast(FP8X4),
+                            rhs_scale=planes[z],
+                            start=(z == 0),
+                            stop=(z == PASSES - 1),
+                        )
+                h.append(view)
+            first = keep.tile([P, count, width], F32, name="first" + name)
+            pair_sum = keep.tile([P, count, width], F32, name="pair_sum" + name)
+            pair_gap = keep.tile([P, count, width], F32, name="pair_gap" + name)
+            third_gap = keep.tile([P, count, width], F32, name="third_gap" + name)
+            rows = slice(halves[0], halves[0] + count)
+            m_cols = slice(start // PACK, (start + width) // PACK)
+
+            def square(i, gap, weight):
+                nc.scalar.activation(
+                    squares[i][:, rows, :, m_cols].rearrange("p a t m -> p a m t"),
+                    gap[:].rearrange("p a (m t) -> p a m t", t=PACK),
+                    ACT.Square,
+                    scale=math.sqrt(weight),
+                )
+
+            nc.scalar.copy(first[:], h[0])
+            nc.vector.tensor_tensor(pair_gap[:], h[1], first[:], ALU.subtract)
+            square(0, pair_gap, 1.0 / 6.0)
+            nc.vector.tensor_tensor(pair_sum[:], h[1], first[:], ALU.add)
+            nc.vector.scalar_tensor_tensor(third_gap[:], h[2], -2.0, pair_sum[:], ALU.mult, ALU.add)
+            square(1, third_gap, 1.0 / 18.0)
+            nc.vector.scalar_tensor_tensor(
+                mean_rows[:, rows, start : start + width], third_gap[:], 1.0 / 3.0, h[2], ALU.mult, ALU.add
+            )
+
+        def finish(a, accs):
+            stats = [keep.tile([P, P, PACK], BF16, name="stats%d_%d" % (g, a), align_bytes=64) for g in range(2)]
+            codes = [keep.tile([P, P], U32, name="stat_codes%d_%d" % (g, a), align_bytes=64) for g in range(2)]
+            planes = [keep.tile([P, P], U8, name="stat_planes%d_%d" % (g, a), align_bytes=64) for g in range(2)]
+            var = ring_bank("var%d" % a)[:].rearrange("p (t v) -> p t v", t=PACK)
+            for i in range(2):
+                for t in range(PACK):
+                    nc.tensor.matmul(
+                        var[:, t, :], squares[i][:, a, t, :], identity[:],
+                        start=(i == 0 and t == 0), stop=(i == 1 and t == PACK - 1), is_transpose=True,
+                    )
+            nc.scalar.activation(stats[1][:], var.rearrange("p t v -> p v t"), ACT.Sqrt)
+            means = ring_bank("means%d" % a)[:, : 2 * P].rearrange("p (u v) -> p u v", u=2)
+            pairs = mean_rows[:, a, :].bitcast(F32)
+            for u in range(2):
+                nc.tensor.transpose(means[:, u, :], pairs[:, u : H // 2 : 2], identity[:])
+            nc.vector.tensor_copy(
+                stats[0][:].rearrange("p v t -> p (v t)").bitcast(F32).rearrange("p (v u) -> p v u", u=2),
+                means.rearrange("p u v -> p v u"),
+            )
+            banks = accs()
+            for g in range(2):
+                quantize(codes[g][:], planes[g][:], stats[g][:])
+                for b in range(N // P):
+                    cols = slice(b * P, (b + 1) * P)
+                    nc.tensor.matmul_mx(
+                        out=banks[b][:, :P],
+                        lhsT=last_words[g][:, cols].bitcast(FP8X4),
+                        lhsT_scale=last_planes[4 * g : P, cols],
+                        rhs=codes[g][:].bitcast(FP8X4),
+                        rhs_scale=planes[g][:],
+                        start=(g == 0),
+                        stop=(g == 1),
+                    )
+            results = [keep.tile([P, P], F32, name="result%d_%d" % (a, b)) for b in range(N // P)]
+            cols = slice(a * P, (a + 1) * P)
+            nc.vector.tensor_copy(results[0][:], banks[0][:, :P])
+            nc.sync.dma_start(out[0:P, cols], results[0][:])
+            nc.scalar.copy(results[1][:], banks[1][:, :P])
+            nc.scalar.dma_start(out[P : 2 * P, cols], results[1][:])
+
+        grouped0 = keep.tile([P, PASSES, 128, PACK], BF16, name="grouped0", align_bytes=64)
+        codes0 = placed([P, PASSES, 128], U32, "codes0", 2048)
+        planes0 = keep.tile([P, PASSES, 128], U8, name="planes0", align_bytes=64)
+        for z in range(PASSES):
+            interleave(nc.scalar.copy, grouped0[:, z], raws[(0, z)])
+        quantize(
+            codes0[:].rearrange("p z n -> p (z n)"), planes0[:].rearrange("p z n -> p (z n)"),
+            grouped0[:].rearrange("p z n j -> p (z n) j"),
+        )
+        grouped1 = [
+            keep.tile([P, 128, PACK], BF16, name="grouped1_0", align_bytes=64),
+            placed([P, 128, PACK], BF16, "grouped1_1", 3072),
+        ]
+        codes1 = [placed([P, 128], U32, "codes1_%d" % z, 4096 + 512 * z) for z in range(PASSES)]
+        planes1 = [keep.tile([P, 128], U8, name="planes1_%d" % z, align_bytes=64) for z in range(PASSES)]
+        interleave(nc.scalar.copy, grouped1[0][:], raws[(1, 0)])
+        interleave(nc.vector.tensor_copy, grouped1[1][:], raws[(1, 1)])
+        for z in range(PASSES):
+            quantize(codes1[z][:], planes1[z][:], grouped1[z][:])
+        pool_stats("0", [codes0[:, z, :] for z in range(PASSES)], [planes0[:, z, :] for z in range(PASSES)], 0, 128, (0, 1))
+        codes2 = [placed([P, 256], U32, "codes2_%d" % z, 5120 + 1024 * z) for z in range(PASSES)]
+        planes2 = [keep.tile([P, 256], U8, name="planes2_%d" % z, align_bytes=64) for z in range(PASSES)]
+        halves20 = [
+            keep.tile([P, 128, PACK], BF16, name="grouped2_0a", align_bytes=64),
+            placed([P, 128, PACK], BF16, "grouped2_0b", 3072),
+        ]
+        interleave(nc.scalar.copy, halves20[0][:], raws[(2, 0)][:, :, :128])
+        interleave(nc.vector.tensor_copy, halves20[1][:], raws[(2, 0)][:, :, 128:])
+        for i in range(2):
+            quantize(codes2[0][:, 128 * i : 128 * (i + 1)], planes2[0][:, 128 * i : 128 * (i + 1)], halves20[i][:])
+        pool_stats("1", [t[:] for t in codes1], [t[:] for t in planes1], 128, 128, (0, 1))
+        grouped21 = placed([P, 256, PACK], BF16, "grouped2_1", 1024)
+        for i in range(2):
+            interleave(nc.scalar.copy, grouped21[:, 128 * i : 128 * (i + 1)], raws[(2, 1)][:, :, 128 * i : 128 * (i + 1)])
+        quantize(codes2[1][:], planes2[1][:], grouped21[:])
+        for a in range(HALVES):
+            pool_stats("2_%d" % a, [t[:] for t in codes2], [t[:] for t in planes2], 256, 256, (a,))
+        finish(0, lambda: [psum.tile([P, BANK], F32, name="acc0_%d" % b) for b in range(N // P)])
+        finish(1, lambda: [ring_bank("acc1_%d" % b) for b in range(N // P)])

@@ -36,58 +36,59 @@ def tile_picked_statpool_none_p_kernel(
         def placed(shape, dtype, name, offset):
             return shared.tile(shape, dtype, name=name, align_bytes=64, offset=offset)
 
-        def ring_bank(name):
-            return psum.tile([P, BANK], F32, name=name, tag="ring", bufs=6)
+        def bank(number, name):
+            return psum.tile([P, BANK], F32, name=name, tag="bank%d" % number)
 
         offsets = keep.tile([P, S // 16], U16, name="offsets")
         nc.sync.dma_start(offsets[:], offs)
 
-        x_tiles = [keep.tile([P, T], I32, name="x_tile0", align_bytes=64), placed([P, T], I32, "x_tile1", 2048)]
-        nc.sync.dma_start(x_tiles[0][:], x_words[0].rearrange("p n t -> p (n t)").bitcast(I32))
-
         x_planes = keep.tile([P, T], U8, name="x_planes", tag="planes", align_bytes=64)
         nc.gpsimd.memset(x_planes[:].bitcast(I32), 0)
-        for q in range(4):
+        for q in range(2):
             nc.sync.dma_start(
                 x_planes[32 * q : 32 * q + 4 * PASSES, :].bitcast(I32),
                 x_scales[:, 4 * q : 4 * q + 4, :].bitcast(I32),
             )
+        for q in range(2, 4):
+            for z in range(PASSES):
+                nc.sync.dma_start(
+                    x_planes[32 * q + 4 * z : 32 * q + 4 * z + 4, :].bitcast(I32),
+                    x_scales[z, 4 * q : 4 * q + 4, :].bitcast(I32),
+                )
 
-        zeros = placed([P, P], F32, "zeros", 2048 + 4 * T - 256)
+        zeros = placed([P, T + P], F32, "zeros", 4 * T - 256)
         identity = keep.tile([P, P], F32, name="identity")
-        nc.gpsimd.memset(zeros[:], 0.0)
+        nc.vector.memset(zeros[:, :P], 0.0)
         nc.gpsimd.affine_select(
-            out=identity[:], in_=zeros[:], compare_op=ALU.not_equal, fill=1.0, base=0, pattern=[[-1, P]], channel_multiplier=1
+            out=identity[:], in_=zeros[:, :P], compare_op=ALU.not_equal, fill=1.0, base=0, pattern=[[-1, P]], channel_multiplier=1
         )
         warm = keep.tile([P, 1], F32, name="warm")
         nc.scalar.activation(warm[:], identity[:, 0:1], ACT.Sqrt)
 
-        nc.sync.dma_start(x_tiles[1][:], x_words[1].rearrange("p n t -> p (n t)").bitcast(I32))
-        raw_all = placed([P, PASSES * PACK * H], F32, "raw_all", 2048 + 4 * T)
-        chunks = ((0, 128), (128, 128), (256, 256))
+        x_tiles = [placed([P, T], I32, "x_tile%d" % z, 4 * T * z) for z in range(PASSES)]
+        for z in range(PASSES):
+            nc.sync.dma_start(x_tiles[z][:], x_words[z].rearrange("p n t -> p (n t)").bitcast(I32))
+        raw_all = placed([P, PASSES * PACK * H], F32, "raw_all", 8 * T)
+        pieces = ((0, 0), (0, 1), (1, 0), (1, 1), (2, 0), (3, 0), (2, 1), (3, 1))
         raws = {}
-        for c, (start, width) in enumerate(chunks):
-            for z in range(PASSES):
-                at = PACK * (PASSES * start + z * width)
-                raws[(c, z)] = raw_all[:, at : at + PACK * width].rearrange("p (j n) -> p j n", j=PACK)
-                rows = w1[z * P * PACK : (z + 1) * P * PACK, start : start + width]
-                nc.sync.dma_start(raws[(c, z)], rows.rearrange("(p j) n -> p j n", j=PACK))
+        for i, (c, z) in enumerate(pieces):
+            raws[(c, z)] = raw_all[:, i * PACK * P : (i + 1) * PACK * P].rearrange("p (j n) -> p j n", j=PACK)
+            rows = w1[z * P * PACK : (z + 1) * P * PACK, c * P : (c + 1) * P]
+            nc.sync.dma_start(raws[(c, z)], rows.rearrange("(p j) n -> p j n", j=PACK))
 
         picked_planes = keep.tile([P, S], U8, name="picked_planes", align_bytes=64)
         picked = [
             keep.tile([P, S], U32, name="picked0", align_bytes=64),
             keep.tile([P, S], U32, name="picked1", tag="planes", align_bytes=64),
         ]
-        nc.vector.tensor_copy(picked[0][:], x_tiles[0][:].bitcast(U32).indirect(offsets[:]))
         nc.vector.tensor_copy(picked_planes[:], x_planes[:].indirect(offsets[:]))
-        nc.vector.tensor_copy(picked[1][:], x_tiles[1][:].bitcast(U32).indirect(offsets[:]))
+        for z in range(PASSES):
+            nc.vector.tensor_copy(picked[z][:], x_tiles[z][:].bitcast(U32).indirect(offsets[:]))
 
-        last_words = []
+        last_words = placed([P, 2, N], I32, "last_words", 6400)
         for g, words in enumerate((w2_words, w3_words)):
-            tile = placed([P, N], I32, "last_words%d" % g, 7168 + 1024 * g)
-            nc.sync.dma_start(tile[:], words[0].rearrange("p n t -> p (n t)").bitcast(I32))
-            last_words.append(tile)
-        last_planes = placed([P, N], U8, "last_planes", 9216)
+            nc.sync.dma_start(last_words[:, g, :], words[0].rearrange("p n t -> p (n t)").bitcast(I32))
+        last_planes = placed([P, N], U8, "last_planes", 15872)
         nc.gpsimd.memset(last_planes[:].bitcast(I32), 0)
         for g, scales in enumerate((w2_scales, w3_scales)):
             for q in range(4):
@@ -105,11 +106,11 @@ def tile_picked_statpool_none_p_kernel(
         mean_rows = keep.tile([P, HALVES, H], BF16, name="mean_rows", align_bytes=64)
         squares = [keep.tile([P, HALVES, PACK, P], F32, name="squares%d" % i) for i in range(2)]
 
-        def pool_stats(name, codes, planes, start, width, halves):
+        def pool_stats(name, codes, planes, start, width, halves, first_bank):
             count = len(halves)
             h = []
             for d in range(PIECES):
-                view = ring_bank("h%s_%d" % (name, d))[:, : count * width].rearrange("p (a n) -> p a n", a=count)
+                view = bank(first_bank + d, "h%s_%d" % (name, d))[:, : count * width].rearrange("p (a n) -> p a n", a=count)
                 for i, a in enumerate(halves):
                     cols = slice(d * V + a * P, d * V + (a + 1) * P)
                     for z in range(PASSES):
@@ -138,21 +139,21 @@ def tile_picked_statpool_none_p_kernel(
                     scale=math.sqrt(weight),
                 )
 
-            nc.scalar.copy(first[:], h[0])
-            nc.vector.tensor_tensor(pair_gap[:], h[1], first[:], ALU.subtract)
-            square(0, pair_gap, 1.0 / 6.0)
-            nc.vector.tensor_tensor(pair_sum[:], h[1], first[:], ALU.add)
-            nc.vector.scalar_tensor_tensor(third_gap[:], h[2], -2.0, pair_sum[:], ALU.mult, ALU.add)
-            square(1, third_gap, 1.0 / 18.0)
+            nc.scalar.activation(first[:], h[0], ACT.Copy, scale=1.0 / 3.0)
+            nc.vector.scalar_tensor_tensor(pair_sum[:], h[1], 1.0 / 3.0, first[:], ALU.mult, ALU.add)
+            nc.vector.scalar_tensor_tensor(pair_gap[:], h[1], 1.0 / 3.0, first[:], ALU.mult, ALU.subtract)
+            square(0, pair_gap, 3.0 / 2.0)
+            nc.vector.scalar_tensor_tensor(third_gap[:], h[2], -2.0 / 3.0, pair_sum[:], ALU.mult, ALU.add)
+            square(1, third_gap, 1.0 / 2.0)
             nc.vector.scalar_tensor_tensor(
-                mean_rows[:, rows, start : start + width], third_gap[:], 1.0 / 3.0, h[2], ALU.mult, ALU.add
+                mean_rows[:, rows, start : start + width], h[2], 1.0 / 3.0, pair_sum[:], ALU.mult, ALU.add
             )
 
-        def finish(a, accs):
+        def finish(a, var_bank, mean_bank, out_bank, copies, second_queue):
             stats = [keep.tile([P, P, PACK], BF16, name="stats%d_%d" % (g, a), align_bytes=64) for g in range(2)]
             codes = [keep.tile([P, P], U32, name="stat_codes%d_%d" % (g, a), align_bytes=64) for g in range(2)]
             planes = [keep.tile([P, P], U8, name="stat_planes%d_%d" % (g, a), align_bytes=64) for g in range(2)]
-            var = ring_bank("var%d" % a)[:].rearrange("p (t v) -> p t v", t=PACK)
+            var = bank(var_bank, "var%d" % a)[:].rearrange("p (t v) -> p t v", t=PACK)
             for i in range(2):
                 for t in range(PACK):
                     nc.tensor.matmul(
@@ -160,7 +161,7 @@ def tile_picked_statpool_none_p_kernel(
                         start=(i == 0 and t == 0), stop=(i == 1 and t == PACK - 1), is_transpose=True,
                     )
             nc.scalar.activation(stats[1][:], var.rearrange("p t v -> p v t"), ACT.Sqrt)
-            means = ring_bank("means%d" % a)[:, : 2 * P].rearrange("p (u v) -> p u v", u=2)
+            means = bank(mean_bank, "means%d" % a)[:, : 2 * P].rearrange("p (u v) -> p u v", u=2)
             pairs = mean_rows[:, a, :].bitcast(F32)
             for u in range(2):
                 nc.tensor.transpose(means[:, u, :], pairs[:, u : H // 2 : 2], identity[:])
@@ -168,14 +169,14 @@ def tile_picked_statpool_none_p_kernel(
                 stats[0][:].rearrange("p v t -> p (v t)").bitcast(F32).rearrange("p (v u) -> p v u", u=2),
                 means.rearrange("p u v -> p v u"),
             )
-            banks = accs()
+            banks = [bank(out_bank + b, "acc%d_%d" % (a, b)) for b in range(N // P)]
             for g in range(2):
                 quantize(codes[g][:], planes[g][:], stats[g][:])
                 for b in range(N // P):
                     cols = slice(b * P, (b + 1) * P)
                     nc.tensor.matmul_mx(
                         out=banks[b][:, :P],
-                        lhsT=last_words[g][:, cols].bitcast(FP8X4),
+                        lhsT=last_words[:, g, cols].bitcast(FP8X4),
                         lhsT_scale=last_planes[4 * g : P, cols],
                         rhs=codes[g][:].bitcast(FP8X4),
                         rhs_scale=planes[g][:],
@@ -184,47 +185,29 @@ def tile_picked_statpool_none_p_kernel(
                     )
             results = [keep.tile([P, P], F32, name="result%d_%d" % (a, b)) for b in range(N // P)]
             cols = slice(a * P, (a + 1) * P)
-            nc.vector.tensor_copy(results[0][:], banks[0][:, :P])
+            copies[0](results[0][:], banks[0][:, :P])
             nc.sync.dma_start(out[0:P, cols], results[0][:])
-            nc.scalar.copy(results[1][:], banks[1][:, :P])
-            nc.scalar.dma_start(out[P : 2 * P, cols], results[1][:])
+            copies[1](results[1][:], banks[1][:, :P])
+            second_queue.dma_start(out[P : 2 * P, cols], results[1][:])
 
-        grouped0 = keep.tile([P, PASSES, 128, PACK], BF16, name="grouped0", align_bytes=64)
-        codes0 = placed([P, PASSES, 128], U32, "codes0", 2048)
-        planes0 = keep.tile([P, PASSES, 128], U8, name="planes0", align_bytes=64)
-        for z in range(PASSES):
-            interleave(nc.scalar.copy, grouped0[:, z], raws[(0, z)])
-        quantize(
-            codes0[:].rearrange("p z n -> p (z n)"), planes0[:].rearrange("p z n -> p (z n)"),
-            grouped0[:].rearrange("p z n j -> p (z n) j"),
-        )
-        grouped1 = [
-            keep.tile([P, 128, PACK], BF16, name="grouped1_0", align_bytes=64),
-            placed([P, 128, PACK], BF16, "grouped1_1", 3072),
-        ]
-        codes1 = [placed([P, 128], U32, "codes1_%d" % z, 4096 + 512 * z) for z in range(PASSES)]
-        planes1 = [keep.tile([P, 128], U8, name="planes1_%d" % z, align_bytes=64) for z in range(PASSES)]
-        interleave(nc.scalar.copy, grouped1[0][:], raws[(1, 0)])
-        interleave(nc.vector.tensor_copy, grouped1[1][:], raws[(1, 1)])
-        for z in range(PASSES):
-            quantize(codes1[z][:], planes1[z][:], grouped1[z][:])
-        pool_stats("0", [codes0[:, z, :] for z in range(PASSES)], [planes0[:, z, :] for z in range(PASSES)], 0, 128, (0, 1))
-        codes2 = [placed([P, 256], U32, "codes2_%d" % z, 5120 + 1024 * z) for z in range(PASSES)]
-        planes2 = [keep.tile([P, 256], U8, name="planes2_%d" % z, align_bytes=64) for z in range(PASSES)]
-        halves20 = [
-            keep.tile([P, 128, PACK], BF16, name="grouped2_0a", align_bytes=64),
-            placed([P, 128, PACK], BF16, "grouped2_0b", 3072),
-        ]
-        interleave(nc.scalar.copy, halves20[0][:], raws[(2, 0)][:, :, :128])
-        interleave(nc.vector.tensor_copy, halves20[1][:], raws[(2, 0)][:, :, 128:])
-        for i in range(2):
-            quantize(codes2[0][:, 128 * i : 128 * (i + 1)], planes2[0][:, 128 * i : 128 * (i + 1)], halves20[i][:])
-        pool_stats("1", [t[:] for t in codes1], [t[:] for t in planes1], 128, 128, (0, 1))
-        grouped21 = placed([P, 256, PACK], BF16, "grouped2_1", 1024)
-        for i in range(2):
-            interleave(nc.scalar.copy, grouped21[:, 128 * i : 128 * (i + 1)], raws[(2, 1)][:, :, 128 * i : 128 * (i + 1)])
-        quantize(codes2[1][:], planes2[1][:], grouped21[:])
-        for a in range(HALVES):
-            pool_stats("2_%d" % a, [t[:] for t in codes2], [t[:] for t in planes2], 256, 256, (a,))
-        finish(0, lambda: [psum.tile([P, BANK], F32, name="acc0_%d" % b) for b in range(N // P)])
-        finish(1, lambda: [ring_bank("acc1_%d" % b) for b in range(N // P)])
+        codes = placed([P, PASSES, H], U32, "w1_codes", 8448)
+        planes = keep.tile([P, PASSES, H], U8, name="w1_planes", align_bytes=64)
+        on_vector = ((1, 1), (3, 0), (3, 1))
+        for c, z in pieces:
+            cols = slice(c * P, (c + 1) * P)
+            if (c, z) in on_vector:
+                grouped = placed([P, P, PACK], BF16, "grouped%d_%d" % (c, z), 12544 + 1024 * on_vector.index((c, z)))
+                interleave(nc.vector.tensor_copy, grouped[:], raws[(c, z)])
+            else:
+                grouped = keep.tile([P, P, PACK], BF16, name="grouped%d_%d" % (c, z), align_bytes=64)
+                interleave(nc.scalar.copy, grouped[:], raws[(c, z)])
+            quantize(codes[:, z, cols], planes[:, z, cols], grouped[:])
+        units = (("0", 0, 128, (0, 1), 0), ("1", 128, 128, (0, 1), 3), ("2", 256, 256, (0,), 0), ("3", 256, 256, (1,), 3))
+        for name, start, width, halves, first_bank in units:
+            cols = slice(start, start + width)
+            pool_stats(
+                name, [codes[:, z, cols] for z in range(PASSES)], [planes[:, z, cols] for z in range(PASSES)],
+                start, width, halves, first_bank,
+            )
+        finish(0, 6, 7, 0, (nc.scalar.copy, nc.scalar.copy), nc.sync)
+        finish(1, 2, 3, 4, (nc.vector.tensor_copy, nc.scalar.copy), nc.scalar)

@@ -39,10 +39,15 @@ def tile_picked_statpool_none_p_kernel(
         def bank(number, name):
             return psum.tile([P, BANK], F32, name=name, tag="bank%d" % number)
 
+        def w1_rows(z, cols):
+            return w1[z * P * PACK : (z + 1) * P * PACK, cols].rearrange("(p j) n -> p j n", j=PACK)
+
         offsets = keep.tile([P, S // 16], U16, name="offsets")
         nc.sync.dma_start(offsets[:], offs)
+        raw0a = keep.tile([P, PACK, H // 2], F32, name="raw0a", align_bytes=64)
+        nc.sync.dma_start(raw0a[:], w1_rows(0, slice(0, H // 2)))
 
-        x_planes = keep.tile([P, T], U8, name="x_planes", tag="planes", align_bytes=64)
+        x_planes = keep.tile([P, T], U8, name="x_planes", align_bytes=64)
         nc.gpsimd.memset(x_planes[:].bitcast(I32), 0)
         for q in range(2):
             nc.sync.dma_start(
@@ -56,39 +61,81 @@ def tile_picked_statpool_none_p_kernel(
                     x_scales[z, 4 * q : 4 * q + 4, :].bitcast(I32),
                 )
 
-        zeros = placed([P, T + P], F32, "zeros", 4 * T - 256)
-        identity = keep.tile([P, P], F32, name="identity")
-        nc.vector.memset(zeros[:, :P], 0.0)
-        nc.gpsimd.affine_select(
-            out=identity[:], in_=zeros[:, :P], compare_op=ALU.not_equal, fill=1.0, base=0, pattern=[[-1, P]], channel_multiplier=1
-        )
+        warm_in = placed([P, 4128], F32, "warm_in", 4096 - 64)
         warm = keep.tile([P, 1], F32, name="warm")
-        nc.scalar.activation(warm[:], identity[:, 0:1], ACT.Sqrt)
+        nc.vector.memset(warm_in[:, 0:1], 1.0)
+        nc.scalar.activation(warm[:], warm_in[:, 0:1], ACT.Sqrt)
 
-        x_tiles = [placed([P, T], I32, "x_tile%d" % z, 4 * T * z) for z in range(PASSES)]
-        for z in range(PASSES):
-            nc.sync.dma_start(x_tiles[z][:], x_words[z].rearrange("p n t -> p (n t)").bitcast(I32))
-        raw_all = placed([P, PASSES * PACK * H], F32, "raw_all", 8 * T)
-        pieces = ((0, 0), (0, 1), (1, 0), (1, 1), (2, 0), (3, 0), (2, 1), (3, 1))
-        raws = {}
-        for i, (c, z) in enumerate(pieces):
-            raws[(c, z)] = raw_all[:, i * PACK * P : (i + 1) * PACK * P].rearrange("p (j n) -> p j n", j=PACK)
-            rows = w1[z * P * PACK : (z + 1) * P * PACK, c * P : (c + 1) * P]
-            nc.sync.dma_start(raws[(c, z)], rows.rearrange("(p j) n -> p j n", j=PACK))
+        raw0b = placed([P, PACK, H // 2], F32, "raw0b", 0)
+        x_tiles = [placed([P, T], I32, "x_tile0", 4096), placed([P, T], I32, "x_tile1", 20480)]
+        raw1 = placed([P, PACK, H], F32, "raw1", 12288)
+        nc.sync.dma_start(raw0b[:], w1_rows(0, slice(H // 2, H)))
+        nc.sync.dma_start(x_tiles[0][:], x_words[0].rearrange("p n t -> p (n t)").bitcast(I32))
+        nc.sync.dma_start(raw1[:], w1_rows(1, slice(0, H)))
+        nc.sync.dma_start(x_tiles[1][:], x_words[1].rearrange("p n t -> p (n t)").bitcast(I32))
 
+        def interleave(copy, grouped, m0, m1, raw, first_m):
+            copy(
+                grouped[:, :, m0:m1, :].rearrange("p t m j -> p m t j"),
+                raw[:, :, PACK * (m0 - first_m) : PACK * (m1 - first_m)].rearrange("p j (m t) -> p m t j", t=PACK),
+            )
+
+        def quantize(codes, planes, values):
+            nc.vector.quantize_mx(out=codes.bitcast(FP8X4), scales=planes, in_=values)
+
+        codes = [keep.tile([P, H], U32, name="w1_codes%d" % z, align_bytes=64) for z in range(PASSES)]
+        planes = [keep.tile([P, H], U8, name="w1_planes%d" % z, align_bytes=64) for z in range(PASSES)]
+
+        grouped0 = keep.tile([P, PACK, P, PACK], BF16, name="grouped0", tag="stage0", align_bytes=64)
+        interleave(nc.scalar.copy, grouped0, 0, 32, raw0a, 0)
+        interleave(nc.vector.tensor_copy, grouped0, 32, 64, raw0a, 0)
         picked_planes = keep.tile([P, S], U8, name="picked_planes", align_bytes=64)
-        picked = [
-            keep.tile([P, S], U32, name="picked0", align_bytes=64),
-            keep.tile([P, S], U32, name="picked1", tag="planes", align_bytes=64),
-        ]
         nc.vector.tensor_copy(picked_planes[:], x_planes[:].indirect(offsets[:]))
-        for z in range(PASSES):
-            nc.vector.tensor_copy(picked[z][:], x_tiles[z][:].bitcast(U32).indirect(offsets[:]))
+        interleave(nc.scalar.copy, grouped0, 64, 96, raw0b, 64)
+        interleave(nc.vector.tensor_copy, grouped0, 96, 128, raw0b, 64)
+        quantize(codes[0][:], planes[0][:], grouped0[:].rearrange("p t m j -> p (t m j)"))
+        picked0 = keep.tile([P, S], U32, name="picked0", tag="stage0", align_bytes=64)
+        nc.vector.tensor_copy(picked0[:], x_tiles[0][:].bitcast(U32).indirect(offsets[:]))
 
-        last_words = placed([P, 2, N], I32, "last_words", 6400)
+        h = {}
+        for a in range(HALVES):
+            for d in range(PIECES):
+                h[(d, a)] = bank(PIECES * a + d, "h%d_%d" % (d, a))[:].rearrange("p (t v) -> p t v", t=PACK)
+
+        def product(z, picked, d, a):
+            cols = slice(d * V + a * P, d * V + (a + 1) * P)
+            for t in range(PACK):
+                nc.tensor.matmul_mx(
+                    out=h[(d, a)][:, t, :],
+                    lhsT=codes[z][:, t * P : (t + 1) * P].bitcast(FP8X4),
+                    lhsT_scale=planes[z][:, t * P : (t + 1) * P],
+                    rhs=picked[:, cols].bitcast(FP8X4),
+                    rhs_scale=picked_planes[4 * z : P, cols],
+                    start=(z == 0 and t == 0),
+                    stop=(z == PASSES - 1 and t == PACK - 1),
+                )
+
+        for d in range(PIECES):
+            for a in range(HALVES):
+                product(0, picked0, d, a)
+
+        grouped1 = placed([P, PACK, P, PACK], BF16, "grouped1", 4096)
+        interleave(nc.scalar.copy, grouped1, 0, 32, raw1, 0)
+        interleave(nc.vector.tensor_copy, grouped1, 32, 128, raw1, 0)
+        quantize(codes[1][:], planes[1][:], grouped1[:].rearrange("p t m j -> p (t m j)"))
+        picked1 = placed([P, S], U32, "picked1", 4096)
+        for d in range(PIECES):
+            nc.vector.tensor_copy(
+                picked1[:, d * V : (d + 1) * V],
+                x_tiles[1][:].bitcast(U32).indirect(offsets[:, d * V // 16 : (d + 1) * V // 16]),
+            )
+            for a in range(HALVES):
+                product(1, picked1, d, a)
+
+        last_words = placed([P, 2, N], I32, "last_words", 8192)
         for g, words in enumerate((w2_words, w3_words)):
             nc.sync.dma_start(last_words[:, g, :], words[0].rearrange("p n t -> p (n t)").bitcast(I32))
-        last_planes = placed([P, N], U8, "last_planes", 15872)
+        last_planes = placed([P, N], U8, "last_planes", 10240)
         nc.gpsimd.memset(last_planes[:].bitcast(I32), 0)
         for g, scales in enumerate((w2_scales, w3_scales)):
             for q in range(4):
@@ -97,89 +144,48 @@ def tile_picked_statpool_none_p_kernel(
                     scales[0, 4 * q : 4 * q + 4, :].bitcast(I32),
                 )
 
-        def interleave(copy, grouped, raw):
-            copy(grouped.rearrange("p (b i) j -> p b j i", i=4), raw.rearrange("p j (b i) -> p b j i", i=4))
+        stats = [[keep.tile([P, P, PACK], BF16, name="stats%d_%d" % (g, a), align_bytes=64) for a in range(HALVES)] for g in range(2)]
+        units = ((0, 0, 128), (1, 0, 128))
+        made = {}
 
-        def quantize(codes, planes, values):
-            nc.vector.quantize_mx(out=codes.bitcast(FP8X4), scales=planes, in_=values.rearrange("p n j -> p (n j)"))
+        def gaps(i):
+            a, v0, v1 = units[i]
+            rows = [h[(d, a)][:, :, v0:v1].rearrange("p t v -> p v t") for d in range(PIECES)]
+            names = ("first", "pair_sum", "pair_gap", "third_gap", "pair_square", "third_square")
+            first, pair_sum, pair_gap, third_gap, pair_square, third_square = [
+                keep.tile([P, v1 - v0, PACK], F32, name="%s%d" % (name, i)) for name in names
+            ]
+            nc.scalar.activation(first[:], rows[0], ACT.Copy, scale=1.0 / 3.0)
+            nc.vector.scalar_tensor_tensor(pair_sum[:], rows[1], 1.0 / 3.0, first[:], ALU.mult, ALU.add)
+            nc.vector.scalar_tensor_tensor(pair_gap[:], rows[1], 1.0 / 3.0, first[:], ALU.mult, ALU.subtract)
+            nc.scalar.activation(pair_square[:], pair_gap[:], ACT.Square, scale=math.sqrt(3.0 / 2.0))
+            nc.vector.scalar_tensor_tensor(third_gap[:], rows[2], -2.0 / 3.0, pair_sum[:], ALU.mult, ALU.add)
+            nc.scalar.activation(third_square[:], third_gap[:], ACT.Square, scale=math.sqrt(1.0 / 2.0))
+            made[i] = (rows[2], pair_sum, pair_square, third_square)
 
-        mean_rows = keep.tile([P, HALVES, H], BF16, name="mean_rows", align_bytes=64)
-        squares = [keep.tile([P, HALVES, PACK, P], F32, name="squares%d" % i) for i in range(2)]
+        def deviation(i, engine):
+            a, v0, v1 = units[i]
+            variance = keep.tile([P, v1 - v0, PACK], F32, name="variance%d" % i)
+            engine.tensor_tensor(variance[:], made[i][2][:], made[i][3][:], ALU.add)
+            nc.scalar.activation(stats[1][a][:, v0:v1, :], variance[:], ACT.Sqrt)
 
-        def pool_stats(name, codes, planes, start, width, halves, first_bank):
-            count = len(halves)
-            h = []
-            for d in range(PIECES):
-                view = bank(first_bank + d, "h%s_%d" % (name, d))[:, : count * width].rearrange("p (a n) -> p a n", a=count)
-                for i, a in enumerate(halves):
-                    cols = slice(d * V + a * P, d * V + (a + 1) * P)
-                    for z in range(PASSES):
-                        nc.tensor.matmul_mx(
-                            out=view[:, i, :],
-                            lhsT=picked[z][:, cols].bitcast(FP8X4),
-                            lhsT_scale=picked_planes[4 * z : P, cols],
-                            rhs=codes[z].bitcast(FP8X4),
-                            rhs_scale=planes[z],
-                            start=(z == 0),
-                            stop=(z == PASSES - 1),
-                        )
-                h.append(view)
-            first = keep.tile([P, count, width], F32, name="first" + name)
-            pair_sum = keep.tile([P, count, width], F32, name="pair_sum" + name)
-            pair_gap = keep.tile([P, count, width], F32, name="pair_gap" + name)
-            third_gap = keep.tile([P, count, width], F32, name="third_gap" + name)
-            rows = slice(halves[0], halves[0] + count)
-            m_cols = slice(start // PACK, (start + width) // PACK)
+        def mean(i):
+            a, v0, v1 = units[i]
+            nc.vector.scalar_tensor_tensor(stats[0][a][:, v0:v1, :], made[i][0], 1.0 / 3.0, made[i][1][:], ALU.mult, ALU.add)
 
-            def square(i, gap, weight):
-                nc.scalar.activation(
-                    squares[i][:, rows, :, m_cols].rearrange("p a t m -> p a m t"),
-                    gap[:].rearrange("p a (m t) -> p a m t", t=PACK),
-                    ACT.Square,
-                    scale=math.sqrt(weight),
-                )
-
-            nc.scalar.activation(first[:], h[0], ACT.Copy, scale=1.0 / 3.0)
-            nc.vector.scalar_tensor_tensor(pair_sum[:], h[1], 1.0 / 3.0, first[:], ALU.mult, ALU.add)
-            nc.vector.scalar_tensor_tensor(pair_gap[:], h[1], 1.0 / 3.0, first[:], ALU.mult, ALU.subtract)
-            square(0, pair_gap, 3.0 / 2.0)
-            nc.vector.scalar_tensor_tensor(third_gap[:], h[2], -2.0 / 3.0, pair_sum[:], ALU.mult, ALU.add)
-            square(1, third_gap, 1.0 / 2.0)
-            nc.vector.scalar_tensor_tensor(
-                mean_rows[:, rows, start : start + width], h[2], 1.0 / 3.0, pair_sum[:], ALU.mult, ALU.add
-            )
-
-        def finish(a, var_bank, mean_bank, out_bank, copies, second_queue):
-            stats = [keep.tile([P, P, PACK], BF16, name="stats%d_%d" % (g, a), align_bytes=64) for g in range(2)]
-            codes = [keep.tile([P, P], U32, name="stat_codes%d_%d" % (g, a), align_bytes=64) for g in range(2)]
-            planes = [keep.tile([P, P], U8, name="stat_planes%d_%d" % (g, a), align_bytes=64) for g in range(2)]
-            var = bank(var_bank, "var%d" % a)[:].rearrange("p (t v) -> p t v", t=PACK)
-            for i in range(2):
-                for t in range(PACK):
-                    nc.tensor.matmul(
-                        var[:, t, :], squares[i][:, a, t, :], identity[:],
-                        start=(i == 0 and t == 0), stop=(i == 1 and t == PACK - 1), is_transpose=True,
-                    )
-            nc.scalar.activation(stats[1][:], var.rearrange("p t v -> p v t"), ACT.Sqrt)
-            means = bank(mean_bank, "means%d" % a)[:, : 2 * P].rearrange("p (u v) -> p u v", u=2)
-            pairs = mean_rows[:, a, :].bitcast(F32)
-            for u in range(2):
-                nc.tensor.transpose(means[:, u, :], pairs[:, u : H // 2 : 2], identity[:])
-            nc.vector.tensor_copy(
-                stats[0][:].rearrange("p v t -> p (v t)").bitcast(F32).rearrange("p (v u) -> p v u", u=2),
-                means.rearrange("p u v -> p v u"),
-            )
-            banks = [bank(out_bank + b, "acc%d_%d" % (a, b)) for b in range(N // P)]
+        def finish(a, banks, copies, second_queue):
             for g in range(2):
-                quantize(codes[g][:], planes[g][:], stats[g][:])
+                stat_codes = keep.tile([P, P], U32, name="stat_codes%d_%d" % (g, a), align_bytes=64)
+                stat_planes = keep.tile([P, P], U8, name="stat_planes%d_%d" % (g, a), align_bytes=64)
+                quantize(stat_codes[:], stat_planes[:], stats[g][a][:].rearrange("p v t -> p (v t)"))
                 for b in range(N // P):
                     cols = slice(b * P, (b + 1) * P)
                     nc.tensor.matmul_mx(
                         out=banks[b][:, :P],
                         lhsT=last_words[:, g, cols].bitcast(FP8X4),
                         lhsT_scale=last_planes[4 * g : P, cols],
-                        rhs=codes[g][:].bitcast(FP8X4),
-                        rhs_scale=planes[g][:],
+                        rhs=stat_codes[:].bitcast(FP8X4),
+                        rhs_scale=stat_planes[:],
                         start=(g == 0),
                         stop=(g == 1),
                     )
@@ -190,24 +196,11 @@ def tile_picked_statpool_none_p_kernel(
             copies[1](results[1][:], banks[1][:, :P])
             second_queue.dma_start(out[P : 2 * P, cols], results[1][:])
 
-        codes = placed([P, PASSES, H], U32, "w1_codes", 8448)
-        planes = keep.tile([P, PASSES, H], U8, name="w1_planes", align_bytes=64)
-        on_vector = ((1, 1), (3, 0), (3, 1))
-        for c, z in pieces:
-            cols = slice(c * P, (c + 1) * P)
-            if (c, z) in on_vector:
-                grouped = placed([P, P, PACK], BF16, "grouped%d_%d" % (c, z), 12544 + 1024 * on_vector.index((c, z)))
-                interleave(nc.vector.tensor_copy, grouped[:], raws[(c, z)])
-            else:
-                grouped = keep.tile([P, P, PACK], BF16, name="grouped%d_%d" % (c, z), align_bytes=64)
-                interleave(nc.scalar.copy, grouped[:], raws[(c, z)])
-            quantize(codes[:, z, cols], planes[:, z, cols], grouped[:])
-        units = (("0", 0, 128, (0, 1), 0), ("1", 128, 128, (0, 1), 3), ("2", 256, 256, (0,), 0), ("3", 256, 256, (1,), 3))
-        for name, start, width, halves, first_bank in units:
-            cols = slice(start, start + width)
-            pool_stats(
-                name, [codes[:, z, cols] for z in range(PASSES)], [planes[:, z, cols] for z in range(PASSES)],
-                start, width, halves, first_bank,
-            )
-        finish(0, 6, 7, 0, (nc.scalar.copy, nc.scalar.copy), nc.sync)
-        finish(1, 2, 3, 4, (nc.vector.tensor_copy, nc.scalar.copy), nc.scalar)
+        for i in range(len(units)):
+            gaps(i)
+        for i in range(len(units)):
+            deviation(i, nc.vector)
+        for i in range(len(units)):
+            mean(i)
+        finish(0, [bank(6, "acc0_0"), bank(7, "acc0_1")], (nc.scalar.copy, nc.scalar.copy), nc.sync)
+        finish(1, [bank(0, "acc1_0"), bank(3, "acc1_1")], (nc.vector.tensor_copy, nc.scalar.copy), nc.scalar)

import math
from contextlib import ExitStack

import concourse.mybir as mybir

K, T, S, V, H, N = 1024, 2048, 768, 256, 512, 256
FLOPS = 2 * K * H * S + 2 * 2 * H * N * V

F32 = mybir.dt.float32
BF16 = mybir.dt.bfloat16
I32 = mybir.dt.int32
U32 = mybir.dt.uint32
U16 = mybir.dt.uint16
U8 = mybir.dt.uint8
FP8X4 = mybir.dt.float8_e4m3fn_x4
ACT = mybir.ActivationFunctionType
ALU = mybir.AluOpType

P = 128
PACK = 4
PASSES = K // (P * PACK)
PIECES = S // V
HALVES = V // P
BANK = 512


def tile_picked_statpool_none_p_kernel(
    tc, x_words, x_scales, w1, w2_words, w2_scales, w3_words, w3_scales, offs, out
):
    nc = tc.nc
    with ExitStack() as ctx:
        keep = ctx.enter_context(tc.tile_pool(name="keep", bufs=1))
        shared = ctx.enter_context(tc.tile_pool(name="shared", bufs=1))
        psum = ctx.enter_context(tc.psum_pool(name="psum", bufs=1))

        def placed(shape, dtype, name, offset):
            return shared.tile(shape, dtype, name=name, align_bytes=64, offset=offset)

        def bank(number, name):
            return psum.tile([P, BANK], F32, name=name, tag="bank%d" % number)

        def w1_rows(z, cols):
            return w1[z * P * PACK : (z + 1) * P * PACK, cols].rearrange("(p j) n -> p j n", j=PACK)

        offsets = keep.tile([P, S // 16], U16, name="offsets")
        nc.sync.dma_start(offsets[:], offs)
        raw0a = keep.tile([P, PACK, H // 2], F32, name="raw0a", align_bytes=64)
        nc.sync.dma_start(raw0a[:], w1_rows(0, slice(0, H // 2)))

        x_planes = keep.tile([P, T], U8, name="x_planes", align_bytes=64)
        nc.gpsimd.memset(x_planes[:].bitcast(I32), 0)
        for q in range(2):
            nc.sync.dma_start(
                x_planes[32 * q : 32 * q + 4 * PASSES, :].bitcast(I32),
                x_scales[:, 4 * q : 4 * q + 4, :].bitcast(I32),
            )
        for q in range(2, 4):
            for z in range(PASSES):
                nc.sync.dma_start(
                    x_planes[32 * q + 4 * z : 32 * q + 4 * z + 4, :].bitcast(I32),
                    x_scales[z, 4 * q : 4 * q + 4, :].bitcast(I32),
                )

        warm_in = placed([P, 4128], F32, "warm_in", 4096 - 64)
        warm = keep.tile([P, 1], F32, name="warm")
        nc.vector.memset(warm_in[:, 0:1], 1.0)
        nc.scalar.activation(warm[:], warm_in[:, 0:1], ACT.Sqrt)

        raw0b = placed([P, PACK, H // 2], F32, "raw0b", 0)
        x_tiles = [placed([P, T], I32, "x_tile0", 4096), placed([P, T], I32, "x_tile1", 20480)]
        raw1 = placed([P, PACK, H], F32, "raw1", 12288)
        nc.sync.dma_start(raw0b[:], w1_rows(0, slice(H // 2, H)))
        nc.sync.dma_start(x_tiles[0][:], x_words[0].rearrange("p n t -> p (n t)").bitcast(I32))
        nc.sync.dma_start(raw1[:], w1_rows(1, slice(0, H)))
        nc.sync.dma_start(x_tiles[1][:], x_words[1].rearrange("p n t -> p (n t)").bitcast(I32))

        def interleave(copy, grouped, m0, m1, raw, first_m):
            copy(
                grouped[:, :, m0:m1, :].rearrange("p t m j -> p m t j"),
                raw[:, :, PACK * (m0 - first_m) : PACK * (m1 - first_m)].rearrange("p j (m t) -> p m t j", t=PACK),
            )

        def quantize(codes, planes, values):
            nc.vector.quantize_mx(out=codes.bitcast(FP8X4), scales=planes, in_=values)

        codes = [keep.tile([P, H], U32, name="w1_codes%d" % z, align_bytes=64) for z in range(PASSES)]
        planes = [keep.tile([P, H], U8, name="w1_planes%d" % z, align_bytes=64) for z in range(PASSES)]

        grouped0 = keep.tile([P, PACK, P, PACK], BF16, name="grouped0", tag="stage0", align_bytes=64)
        interleave(nc.scalar.copy, grouped0, 0, 32, raw0a, 0)
        interleave(nc.vector.tensor_copy, grouped0, 32, 64, raw0a, 0)
        picked_planes = keep.tile([P, S], U8, name="picked_planes", align_bytes=64)
        nc.vector.tensor_copy(picked_planes[:], x_planes[:].indirect(offsets[:]))
        interleave(nc.scalar.copy, grouped0, 64, 96, raw0b, 64)
        interleave(nc.vector.tensor_copy, grouped0, 96, 128, raw0b, 64)
        quantize(codes[0][:], planes[0][:], grouped0[:].rearrange("p t m j -> p (t m j)"))
        picked0 = keep.tile([P, S], U32, name="picked0", tag="stage0", align_bytes=64)
        nc.vector.tensor_copy(picked0[:], x_tiles[0][:].bitcast(U32).indirect(offsets[:]))

        h = {}
        for a in range(HALVES):
            for d in range(PIECES):
                h[(d, a)] = bank(PIECES * a + d, "h%d_%d" % (d, a))[:].rearrange("p (t v) -> p t v", t=PACK)

        def product(z, picked, d, a):
            cols = slice(d * V + a * P, d * V + (a + 1) * P)
            for t in range(PACK):
                nc.tensor.matmul_mx(
                    out=h[(d, a)][:, t, :],
                    lhsT=codes[z][:, t * P : (t + 1) * P].bitcast(FP8X4),
                    lhsT_scale=planes[z][:, t * P : (t + 1) * P],
                    rhs=picked[:, cols].bitcast(FP8X4),
                    rhs_scale=picked_planes[4 * z : P, cols],
                    start=(z == 0 and t == 0),
                    stop=(z == PASSES - 1 and t == PACK - 1),
                )

        for d in range(PIECES):
            for a in range(HALVES):
                product(0, picked0, d, a)

        grouped1 = placed([P, PACK, P, PACK], BF16, "grouped1", 4096)
        interleave(nc.scalar.copy, grouped1, 0, 32, raw1, 0)
        interleave(nc.vector.tensor_copy, grouped1, 32, 128, raw1, 0)
        quantize(codes[1][:], planes[1][:], grouped1[:].rearrange("p t m j -> p (t m j)"))
        picked1 = placed([P, S], U32, "picked1", 4096)
        for d in range(PIECES):
            nc.vector.tensor_copy(
                picked1[:, d * V : (d + 1) * V],
                x_tiles[1][:].bitcast(U32).indirect(offsets[:, d * V // 16 : (d + 1) * V // 16]),
            )
            for a in range(HALVES):
                product(1, picked1, d, a)

        last_words = placed([P, 2, N], I32, "last_words", 8192)
        for g, words in enumerate((w2_words, w3_words)):
            nc.sync.dma_start(last_words[:, g, :], words[0].rearrange("p n t -> p (n t)").bitcast(I32))
        last_planes = placed([P, N], U8, "last_planes", 10240)
        nc.gpsimd.memset(last_planes[:].bitcast(I32), 0)
        for g, scales in enumerate((w2_scales, w3_scales)):
            for q in range(4):
                nc.sync.dma_start(
                    last_planes[32 * q + 4 * g : 32 * q + 4 * g + 4, :].bitcast(I32),
                    scales[0, 4 * q : 4 * q + 4, :].bitcast(I32),
                )

        stats = [[keep.tile([P, P, PACK], BF16, name="stats%d_%d" % (g, a), align_bytes=64) for a in range(HALVES)] for g in range(2)]
        units = ((0, 0, 128), (1, 0, 128))
        made = {}

        def gaps(i):
            a, v0, v1 = units[i]
            rows = [h[(d, a)][:, :, v0:v1].rearrange("p t v -> p v t") for d in range(PIECES)]
            names = ("first", "pair_sum", "pair_gap", "third_gap", "pair_square", "third_square")
            first, pair_sum, pair_gap, third_gap, pair_square, third_square = [
                keep.tile([P, v1 - v0, PACK], F32, name="%s%d" % (name, i)) for name in names
            ]
            nc.scalar.activation(first[:], rows[0], ACT.Copy, scale=1.0 / 3.0)
            nc.vector.scalar_tensor_tensor(pair_sum[:], rows[1], 1.0 / 3.0, first[:], ALU.mult, ALU.add)
            nc.vector.scalar_tensor_tensor(pair_gap[:], rows[1], 1.0 / 3.0, first[:], ALU.mult, ALU.subtract)
            nc.scalar.activation(pair_square[:], pair_gap[:], ACT.Square, scale=math.sqrt(3.0 / 2.0))
            nc.vector.scalar_tensor_tensor(third_gap[:], rows[2], -2.0 / 3.0, pair_sum[:], ALU.mult, ALU.add)
            nc.scalar.activation(third_square[:], third_gap[:], ACT.Square, scale=math.sqrt(1.0 / 2.0))
            made[i] = (rows[2], pair_sum, pair_square, third_square)

        def deviation(i, engine):
            a, v0, v1 = units[i]
            variance = keep.tile([P, v1 - v0, PACK], F32, name="variance%d" % i)
            engine.tensor_tensor(variance[:], made[i][2][:], made[i][3][:], ALU.add)
            nc.scalar.activation(stats[1][a][:, v0:v1, :], variance[:], ACT.Sqrt)

        def mean(i):
            a, v0, v1 = units[i]
            nc.vector.scalar_tensor_tensor(stats[0][a][:, v0:v1, :], made[i][0], 1.0 / 3.0, made[i][1][:], ALU.mult, ALU.add)

        def finish(a, banks, copies, second_queue):
            for g in range(2):
                stat_codes = keep.tile([P, P], U32, name="stat_codes%d_%d" % (g, a), align_bytes=64)
                stat_planes = keep.tile([P, P], U8, name="stat_planes%d_%d" % (g, a), align_bytes=64)
                quantize(stat_codes[:], stat_planes[:], stats[g][a][:].rearrange("p v t -> p (v t)"))
                for b in range(N // P):
                    cols = slice(b * P, (b + 1) * P)
                    nc.tensor.matmul_mx(
                        out=banks[b][:, :P],
                        lhsT=last_words[:, g, cols].bitcast(FP8X4),
                        lhsT_scale=last_planes[4 * g : P, cols],
                        rhs=stat_codes[:].bitcast(FP8X4),
                        rhs_scale=stat_planes[:],
                        start=(g == 0),
                        stop=(g == 1),
                    )
            results = [keep.tile([P, P], F32, name="result%d_%d" % (a, b)) for b in range(N // P)]
            cols = slice(a * P, (a + 1) * P)
            copies[0](results[0][:], banks[0][:, :P])
            nc.sync.dma_start(out[0:P, cols], results[0][:])
            copies[1](results[1][:], banks[1][:, :P])
            second_queue.dma_start(out[P : 2 * P, cols], results[1][:])

        for i in range(len(units)):
            gaps(i)
        for i in range(len(units)):
            deviation(i, nc.vector)
        for i in range(len(units)):
            mean(i)
        finish(0, [bank(6, "acc0_0"), bank(7, "acc0_1")], (nc.scalar.copy, nc.scalar.copy), nc.sync)
        finish(1, [bank(0, "acc1_0"), bank(3, "acc1_1")], (nc.vector.tensor_copy, nc.scalar.copy), nc.scalar)
